import numpy as np
import ml_dtypes


def mxq(x, axis, fmt="e4m3"):
    dtype, down = {"e4m3": (ml_dtypes.float8_e4m3fn, 7), "e5m2": (ml_dtypes.float8_e5m2, 14)}[fmt]
    v = np.moveaxis(np.asarray(x, np.float32).astype(ml_dtypes.bfloat16).astype(np.float64), axis, -1)
    blocks = v.reshape(v.shape[:-1] + (-1, 32))
    amax = np.abs(blocks).max(-1, keepdims=True)
    byte = np.maximum(np.where(amax > 0, np.frexp(amax)[1] - 1 + 127, 0) - down, 1)
    scale = np.exp2(byte - 127.0)
    codes = (blocks / scale).astype(np.float32).astype(dtype).astype(np.float64)
    return np.moveaxis((codes * scale).reshape(v.shape), -1, axis)


WIDE = False


def mx_kscale(k):
    if not WIDE:
        return np.ones(k)
    levels = np.array([10, -10, 5, -5, 0])
    if k % 512:
        return np.exp2(np.random.permutation(np.resize(levels, k // 32))).repeat(32)
    a = np.empty((k // 512, 16))
    for p in range(k // 512):
        a[p, :8] = np.random.permutation(np.resize(levels, 8))
        for g in range(8):
            far = levels[np.abs(levels - a[p, g]) >= 10]
            a[p, g + 8] = far[np.random.randint(len(far))]
    return np.exp2(a.ravel()).repeat(32)


def f64(x):
    return np.asarray(x).astype(np.float64)


def striped(idx):
    return np.tile(idx.reshape(-1, 16).T, (8, 1)).astype(np.uint16)


def unstriped(offs):
    return offs[:16].T.reshape(-1).astype(np.int64)


K, T, E, C, N = 512, 1024, 16, 128, 256


def by_expert(wq, xq):
    return np.concatenate([wq[e].T @ xq[:, e * C:(e + 1) * C] for e in range(E)], axis=1)


def setup_inputs():
    n = np.random.standard_normal
    s = mx_kscale(K)[:, None]
    first = np.random.permutation(np.repeat(np.arange(E), T // E))
    second = (first + 1 + np.random.permutation(np.repeat(np.arange(E - 1), -(-T // (E - 1)))[:T])) % E
    while np.bincount(second, minlength=E).max() != T // E:
        load = np.bincount(second, minlength=E); hi, lo = int(load.argmax()), int(load.argmin())
        t = np.flatnonzero((second == hi) & (first != lo))[0]; second[t] = lo
    slot_token = np.empty(E * C, np.int64); pos = np.empty((2, T), np.int64); fill = np.zeros(E, np.int64)
    place = np.stack([np.random.permutation(C) for _ in range(E)])
    for r, deal in enumerate((first, second)):
        for t in np.random.permutation(T):
            e = deal[t]; j = e * C + place[e, fill[e]]; fill[e] += 1; slot_token[j] = t; pos[r, t] = j
    g = np.random.uniform(0.2, 0.8, T)
    return {
        "xT": (n((K, T)) * s).astype(np.float32),
        "w": (n((E, K, N)) / np.sqrt(K) / s[None]).astype(np.float32),
        "b": (0.3 * n((N, E))).astype(np.float32),
        "gate": np.stack([np.tile(g, (N, 1)), np.tile(1.0 - g, (N, 1))]).astype(np.float32),
        "offs": striped(slot_token),
        "pos1": striped(pos[0]),
        "pos2": striped(pos[1]),
    }


def reference(xT, w, b, gate, offs, pos1, pos2):
    idx = unstriped(offs)
    xq = mxq(f64(xT)[:, idx], 0, "e4m3")
    y = by_expert(mxq(f64(w), 1, "e4m3"), xq)
    y = y + np.repeat(f64(b), C, axis=1)
    return f64(gate[0]) * y[:, unstriped(pos1)] + f64(gate[1]) * y[:, unstriped(pos2)]

@@ -1,0 +1,200 @@
+import concourse.mybir as mybir
+
+FLOPS = 2 * 2048 * 512 * 256
+
+F32 = mybir.dt.float32
+BF16 = mybir.dt.bfloat16
+U32 = mybir.dt.uint32
+U16 = mybir.dt.uint16
+U8 = mybir.dt.uint8
+FP8X4 = mybir.dt.float8_e4m3fn_x4
+MULT = mybir.AluOpType.mult
+ADD = mybir.AluOpType.add
+IDENTITY = mybir.ActivationFunctionType.Identity
+
+K, T, E, C, N = 512, 1024, 16, 128, 256
+SLOTS = E * C
+VCOLS = [0,0,0,0,0,0,0,0,0,256,0,256,0,256,0,224]
+GCOLS = [0,0,0,0,0,0,0,0,0,0,0,0,0,0,0,0]
+XV = 320
+GATHER_TAGS = (("scales0", "codes0"), ("w_grouped0", "w_grouped1"), ("w_grouped2", "w_grouped3"))
+SLICES = ((0, 768), (768, 768), (1536, 512))
+
+
+def interleave(copy, grouped, raw, lo, hi):
+    if hi > lo:
+        copy(
+            grouped[:, 4 * lo : 4 * hi].rearrange("p (c i t) -> p c t i", i=4, t=4),
+            raw[:, :, lo:hi].rearrange("p t (c i) -> p c t i", i=4),
+        )
+
+
+def tile_routed_moe_kernel(tc, xT, w, b, gate, offs, pos1, pos2, out):
+    nc = tc.nc
+    with (
+        tc.tile_pool(name="lists", bufs=1) as lists,
+        tc.tile_pool(name="keep", bufs=1) as keep,
+        tc.psum_pool(name="psum", bufs=1) as psum,
+    ):
+        offs_t = lists.tile([128, SLOTS // 16], U16, name="offs_t")
+        pos1_t = lists.tile([128, T // 16], U16, name="pos1_t")
+        pos2_t = lists.tile([128, T // 16], U16, name="pos2_t")
+
+        x_codes = keep.tile([128, T], U32, name="x_codes", align_bytes=64)
+        x_scales = keep.tile([128, T], U8, name="x_scales", align_bytes=64)
+        nc.gpsimd.memset(x_scales[:], 0)
+
+        w_raw = [keep.tile([128, 2, 4, N], F32, name=f"w_raw{g}") for g in range(8)]
+
+        def load_w(g, lo, hi):
+            nc.sync.dma_start(
+                out=w_raw[g][:, lo:hi].rearrange("p e t n -> p e (t n)"),
+                in_=w[2 * g + lo : 2 * g + hi].rearrange("e (p t) n -> p e (t n)", t=4),
+            )
+
+        x_raw = [keep.tile([128, 4, 512], F32, name=f"x_raw{i}") for i in range(2)]
+        for i in range(2):
+            nc.sync.dma_start(
+                out=x_raw[i][:],
+                in_=xT.rearrange("(p t) n -> p t n", t=4)[:, :, 512 * i : 512 * (i + 1)],
+            )
+        nc.sync.dma_start(offs_t[:], offs)
+        load_w(0, 0, 1)
+        load_w(0, 1, 2)
+        b_t = [keep.tile([128, 2, 8], F32, name=f"b_t{i}") for i in range(2)]
+        for g in range(1, 8):
+            if g < 6:
+                load_w(g, 0, 2)
+            else:
+                load_w(g, 0, 1)
+                load_w(g, 1, 2)
+            if g in (2, 5):
+                i = (2, 5).index(g)
+                nc.sync.dma_start(out=b_t[i][:], in_=b.rearrange("(h p) e -> p h e", h=2)[:, :, 8 * i : 8 * i + 8])
+            if g == 4:
+                nc.sync.dma_start(pos1_t[:], pos1)
+                nc.sync.dma_start(pos2_t[:], pos2)
+        gates = [[keep.tile([128, T], F32, name=f"gate{r}{h}") for r in range(2)] for h in range(2)]
+        for h in range(2):
+            for r in range(2):
+                nc.sync.dma_start(out=gates[h][r][:], in_=gate[r, 128 * h : 128 * (h + 1), :])
+
+        x_grouped = [keep.tile([128, 2048], BF16, name=f"x_grouped{i}", align_bytes=64) for i in range(2)]
+
+        def interleave_x(i):
+            interleave(nc.vector.tensor_copy, x_grouped[i], x_raw[i], 0, XV)
+            interleave(nc.scalar.copy, x_grouped[i], x_raw[i], XV, 512)
+
+        def quantize_x(i):
+            nc.vector.quantize_mx(
+                out=x_codes[:, 512 * i : 512 * (i + 1)].bitcast(FP8X4),
+                scales=x_scales[:, 512 * i : 512 * (i + 1)],
+                in_=x_grouped[i][:],
+            )
+
+        y = [keep.tile([128, SLOTS], F32, name=f"y{h}") for h in range(2)]
+        s_codes = []
+        s_scales = []
+
+        def gather(s):
+            lo, n = SLICES[s]
+            scales_tag, codes_tag = GATHER_TAGS[s]
+            s_scales.append(keep.tile([128, n], U8, name=f"s_scales{lo}", tag=scales_tag, align_bytes=64))
+            s_codes.append(keep.tile([128, n], U32, name=f"s_codes{lo}", tag=codes_tag, align_bytes=64))
+            cols = offs_t[:, lo // 16 : (lo + n) // 16]
+            nc.vector.tensor_copy(s_scales[s][:], x_scales[:].indirect(cols))
+            nc.vector.tensor_copy(s_codes[s][:], x_codes[:].indirect(cols))
+
+        w_grouped = [keep.tile([128, 2, 1024], BF16, name=f"w_grouped{g}", tag=f"w_grouped{g}", align_bytes=64) for g in range(8)]
+        w_codes = [keep.tile([128, 2, N], U32, name=f"w_codes{g}", align_bytes=64) for g in range(8)]
+        w_scales = [keep.tile([128, 2, N], U8, name=f"w_scales{g}", align_bytes=64) for g in range(8)]
+        sums = [psum.tile([128, 2, 2, C], F32, name=f"sums{g}") for g in range(8)]
+
+        def interleave_w(e):
+            g, j = divmod(e, 2)
+            interleave(nc.vector.tensor_copy, w_grouped[g][:, j], w_raw[g][:, j], 0, VCOLS[e])
+            interleave(nc.gpsimd.tensor_copy, w_grouped[g][:, j], w_raw[g][:, j], VCOLS[e], VCOLS[e] + GCOLS[e])
+            interleave(nc.scalar.copy, w_grouped[g][:, j], w_raw[g][:, j], VCOLS[e] + GCOLS[e], N)
+
+        def quantize_w(g):
+            if g < 7:
+                nc.vector.quantize_mx(
+                    out=w_codes[g][:].rearrange("p e n -> p (e n)").bitcast(FP8X4),
+                    scales=w_scales[g][:].rearrange("p e n -> p (e n)"),
+                    in_=w_grouped[g][:].rearrange("p e k -> p (e k)"),
+                )
+            else:
+                for j in range(2):
+                    nc.vector.quantize_mx(
+                        out=w_codes[g][:, j].bitcast(FP8X4), scales=w_scales[g][:, j], in_=w_grouped[g][:, j]
+                    )
+
+        def multiply(g):
+            for j in range(2):
+                e = 2 * g + j
+                s = [lo <= e * C < lo + n for lo, n in SLICES].index(True)
+                c0 = e * C - SLICES[s][0]
+                for h in range(2):
+                    nc.tensor.matmul_mx(
+                        out=sums[g][:, j, h, :],
+                        lhsT=w_codes[g][:, j, 128 * h : 128 * (h + 1)].bitcast(FP8X4),
+                        lhsT_scale=w_scales[g][:, j, 128 * h : 128 * (h + 1)],
+                        rhs=s_codes[s][:, c0 : c0 + C].bitcast(FP8X4),
+                        rhs_scale=s_scales[s][:, c0 : c0 + C],
+                        start=True,
+                        stop=True,
+                    )
+
+        def empty(g):
+            for h in range(2):
+                for j in range(2):
+                    e = 2 * g + j
+                    nc.scalar.activation(
+                        y[h][:, e * C : (e + 1) * C], sums[g][:, j, h, :], IDENTITY, bias=b_t[e // 8][:, h, e % 8 : e % 8 + 1]
+                    )
+
+        interleave_x(0)
+        interleave_x(1)
+        quantize_x(0)
+        quantize_x(1)
+        for e in range(0, 8):
+            interleave_w(e)
+        gather(0)
+        quantize_w(0)
+        quantize_w(1)
+        gather(1)
+        quantize_w(2)
+        quantize_w(3)
+        gather(2)
+        for e in range(8, 16):
+            interleave_w(e)
+        for g in range(4, 8):
+            quantize_w(g)
+        for g in range(0, 8):
+            multiply(g)
+        for g in range(0, 8):
+            empty(g)
+
+        parts = [[keep.tile([128, T], F32, name=f"part{h}{r}") for r in range(2)] for h in range(2)]
+        result = [keep.tile([128, T], F32, name=f"result{h}") for h in range(2)]
+
+        def combine(h, lo, n):
+            for r, pos_t in enumerate((pos1_t, pos2_t)):
+                nc.vector.tensor_tensor(
+                    parts[h][r][:, lo : lo + n],
+                    y[h][:].indirect(pos_t[:, lo // 16 : (lo + n) // 16]),
+                    gates[h][r][:, lo : lo + n],
+                    MULT,
+                )
+
+        def finish(h, lo, n):
+            cols = slice(lo, lo + n)
+            nc.vector.tensor_tensor(result[h][:, cols], parts[h][0][:, cols], parts[h][1][:, cols], ADD)
+            nc.sync.dma_start(out=out[128 * h : 128 * (h + 1), cols], in_=result[h][:, cols])
+
+        combine(0, 0, 1024)
+        combine(1, 0, 512)
+        finish(0, 0, 1024)
+        combine(1, 512, 512)
+        finish(1, 0, 512)
+        finish(1, 512, 512)

@@ -14,10 +14,12 @@ IDENTITY = mybir.ActivationFunctionType.Identity
 
 K, T, E, C, N = 512, 1024, 16, 128, 256
 SLOTS = E * C
-VCOLS = [0,0,0,0,0,0,0,0,0,256,0,256,0,256,0,224]
+VCOLS = [0,0,0,0,0,0,0,0,256,0,0,0,256,0,128,160]
 GCOLS = [0,0,0,0,0,0,0,0,0,0,0,0,0,0,0,0]
-XV = 320
+X_PARTS = ((0, 512), (512, 256), (768, 256))
+XV = 256
 GATHER_TAGS = (("scales0", "codes0"), ("w_grouped0", "w_grouped1"), ("w_grouped2", "w_grouped3"))
+VECTOR_EMPTIES = ((7, 0),)
 SLICES = ((0, 768), (768, 768), (1536, 512))
 
 
@@ -27,6 +29,10 @@ def interleave(copy, grouped, raw, lo, hi):
             grouped[:, 4 * lo : 4 * hi].rearrange("p (c i t) -> p c t i", i=4, t=4),
             raw[:, :, lo:hi].rearrange("p t (c i) -> p c t i", i=4),
         )
+
+
+def gpsimd_copy(nc):
+    return lambda dst, src: nc.gpsimd.tensor_scalar(dst, src, 1.0, 0.0, MULT, ADD)
 
 
 def tile_routed_moe_kernel(tc, xT, w, b, gate, offs, pos1, pos2, out):
@@ -52,12 +58,9 @@ def tile_routed_moe_kernel(tc, xT, w, b, gate, offs, pos1, pos2, out):
                 in_=w[2 * g + lo : 2 * g + hi].rearrange("e (p t) n -> p e (t n)", t=4),
             )
 
-        x_raw = [keep.tile([128, 4, 512], F32, name=f"x_raw{i}") for i in range(2)]
-        for i in range(2):
-            nc.sync.dma_start(
-                out=x_raw[i][:],
-                in_=xT.rearrange("(p t) n -> p t n", t=4)[:, :, 512 * i : 512 * (i + 1)],
-            )
+        x_raw = [keep.tile([128, 4, n], F32, name=f"x_raw{lo}") for lo, n in X_PARTS]
+        for i, (lo, n) in enumerate(X_PARTS):
+            nc.sync.dma_start(out=x_raw[i][:], in_=xT.rearrange("(p t) n -> p t n", t=4)[:, :, lo : lo + n])
         nc.sync.dma_start(offs_t[:], offs)
         load_w(0, 0, 1)
         load_w(0, 1, 2)
@@ -79,17 +82,17 @@ def tile_routed_moe_kernel(tc, xT, w, b, gate, offs, pos1, pos2, out):
             for r in range(2):
                 nc.sync.dma_start(out=gates[h][r][:], in_=gate[r, 128 * h : 128 * (h + 1), :])
 
-        x_grouped = [keep.tile([128, 2048], BF16, name=f"x_grouped{i}", align_bytes=64) for i in range(2)]
+        x_grouped = [keep.tile([128, 4 * n], BF16, name=f"x_grouped{lo}", align_bytes=64) for lo, n in X_PARTS]
 
         def interleave_x(i):
-            interleave(nc.vector.tensor_copy, x_grouped[i], x_raw[i], 0, XV)
-            interleave(nc.scalar.copy, x_grouped[i], x_raw[i], XV, 512)
+            n = X_PARTS[i][1]
+            interleave(nc.vector.tensor_copy, x_grouped[i], x_raw[i], 0, XV * n // 512)
+            interleave(nc.scalar.copy, x_grouped[i], x_raw[i], XV * n // 512, n)
 
         def quantize_x(i):
+            lo, n = X_PARTS[i]
             nc.vector.quantize_mx(
-                out=x_codes[:, 512 * i : 512 * (i + 1)].bitcast(FP8X4),
-                scales=x_scales[:, 512 * i : 512 * (i + 1)],
-                in_=x_grouped[i][:],
+                out=x_codes[:, lo : lo + n].bitcast(FP8X4), scales=x_scales[:, lo : lo + n], in_=x_grouped[i][:]
             )
 
         y = [keep.tile([128, SLOTS], F32, name=f"y{h}") for h in range(2)]
@@ -113,7 +116,7 @@ def tile_routed_moe_kernel(tc, xT, w, b, gate, offs, pos1, pos2, out):
         def interleave_w(e):
             g, j = divmod(e, 2)
             interleave(nc.vector.tensor_copy, w_grouped[g][:, j], w_raw[g][:, j], 0, VCOLS[e])
-            interleave(nc.gpsimd.tensor_copy, w_grouped[g][:, j], w_raw[g][:, j], VCOLS[e], VCOLS[e] + GCOLS[e])
+            interleave(gpsimd_copy(nc), w_grouped[g][:, j], w_raw[g][:, j], VCOLS[e], VCOLS[e] + GCOLS[e])
             interleave(nc.scalar.copy, w_grouped[g][:, j], w_raw[g][:, j], VCOLS[e] + GCOLS[e], N)
 
         def quantize_w(g):
@@ -145,18 +148,25 @@ def tile_routed_moe_kernel(tc, xT, w, b, gate, offs, pos1, pos2, out):
                         stop=True,
                     )
 
-        def empty(g):
-            for h in range(2):
-                for j in range(2):
-                    e = 2 * g + j
-                    nc.scalar.activation(
-                        y[h][:, e * C : (e + 1) * C], sums[g][:, j, h, :], IDENTITY, bias=b_t[e // 8][:, h, e % 8 : e % 8 + 1]
-                    )
+        def empty(g, h):
+            y_pair = y[h][:, 2 * g * C : 2 * (g + 1) * C]
+            if (g, h) in VECTOR_EMPTIES:
+                nc.vector.tensor_tensor(
+                    y_pair.rearrange("p (e c) -> p e c", c=C),
+                    sums[g][:, :, h, :],
+                    b_t[g // 4][:, h, 2 * g % 8 : 2 * g % 8 + 2].unsqueeze(2).to_broadcast([128, 2, C]),
+                    ADD,
+                )
+                return
+            for j in range(2):
+                e = 2 * g + j
+                nc.scalar.activation(
+                    y[h][:, e * C : (e + 1) * C], sums[g][:, j, h, :], IDENTITY, bias=b_t[g // 4][:, h, e % 8 : e % 8 + 1]
+                )
 
-        interleave_x(0)
-        interleave_x(1)
-        quantize_x(0)
-        quantize_x(1)
+        for i in range(len(X_PARTS)):
+            interleave_x(i)
+            quantize_x(i)
         for e in range(0, 8):
             interleave_w(e)
         gather(0)
@@ -172,8 +182,9 @@ def tile_routed_moe_kernel(tc, xT, w, b, gate, offs, pos1, pos2, out):
             quantize_w(g)
         for g in range(0, 8):
             multiply(g)
-        for g in range(0, 8):
-            empty(g)
+        for h in range(2):
+            for g in range(0, 8):
+                empty(g, h)
 
         parts = [[keep.tile([128, T], F32, name=f"part{h}{r}") for r in range(2)] for h in range(2)]
         result = [keep.tile([128, T], F32, name=f"result{h}") for h in range(2)]

@@ -14,10 +14,10 @@ IDENTITY = mybir.ActivationFunctionType.Identity
 
 K, T, E, C, N = 512, 1024, 16, 128, 256
 SLOTS = E * C
-VCOLS = [0,0,0,0,0,0,0,0,256,0,0,0,256,0,128,160]
-GCOLS = [0,0,0,0,0,0,0,0,0,0,0,0,0,0,0,0]
-X_PARTS = ((0, 512), (512, 256), (768, 256))
-XV = 256
+VCOLS = [0,0,0,0,0,0,0,0,0,0,0,0,0,128,0,160]
+GCOLS = [0,0,256,0,0,0,256,0,0,0,256,0,0,0,0,0]
+X_PARTS = ((0, 512), (512, 512))
+XV = 320
 GATHER_TAGS = (("scales0", "codes0"), ("w_grouped0", "w_grouped1"), ("w_grouped2", "w_grouped3"))
 VECTOR_EMPTIES = ((7, 0),)
 SLICES = ((0, 768), (768, 768), (1536, 512))
@@ -65,18 +65,20 @@ def tile_routed_moe_kernel(tc, xT, w, b, gate, offs, pos1, pos2, out):
         load_w(0, 0, 1)
         load_w(0, 1, 2)
         b_t = [keep.tile([128, 2, 8], F32, name=f"b_t{i}") for i in range(2)]
-        for g in range(1, 8):
-            if g < 6:
-                load_w(g, 0, 2)
-            else:
-                load_w(g, 0, 1)
-                load_w(g, 1, 2)
-            if g in (2, 5):
-                i = (2, 5).index(g)
-                nc.sync.dma_start(out=b_t[i][:], in_=b.rearrange("(h p) e -> p h e", h=2)[:, :, 8 * i : 8 * i + 8])
-            if g == 4:
-                nc.sync.dma_start(pos1_t[:], pos1)
-                nc.sync.dma_start(pos2_t[:], pos2)
+        def load_bias(i):
+            nc.sync.dma_start(out=b_t[i][:], in_=b.rearrange("(h p) e -> p h e", h=2)[:, :, 8 * i : 8 * i + 8])
+
+        for g in range(1, 5):
+            load_w(g, 0, 2)
+        load_bias(0)
+        nc.sync.dma_start(pos1_t[:], pos1)
+        nc.sync.dma_start(pos2_t[:], pos2)
+        load_w(5, 0, 2)
+        load_w(6, 0, 1)
+        load_w(6, 1, 2)
+        load_w(7, 0, 1)
+        load_bias(1)
+        load_w(7, 1, 2)
         gates = [[keep.tile([128, T], F32, name=f"gate{r}{h}") for r in range(2)] for h in range(2)]
         for h in range(2):
             for r in range(2):
@@ -85,9 +87,10 @@ def tile_routed_moe_kernel(tc, xT, w, b, gate, offs, pos1, pos2, out):
         x_grouped = [keep.tile([128, 4 * n], BF16, name=f"x_grouped{lo}", align_bytes=64) for lo, n in X_PARTS]
 
         def interleave_x(i):
-            n = X_PARTS[i][1]
-            interleave(nc.vector.tensor_copy, x_grouped[i], x_raw[i], 0, XV * n // 512)
-            interleave(nc.scalar.copy, x_grouped[i], x_raw[i], XV * n // 512, n)
+            lo, n = X_PARTS[i]
+            part = x_raw[i]
+            interleave(nc.vector.tensor_copy, x_grouped[i], part, 0, XV * n // 512)
+            interleave(nc.scalar.copy, x_grouped[i], part, XV * n // 512, n)
 
         def quantize_x(i):
             lo, n = X_PARTS[i]
@@ -99,14 +102,15 @@ def tile_routed_moe_kernel(tc, xT, w, b, gate, offs, pos1, pos2, out):
         s_codes = []
         s_scales = []
 
-        def gather(s):
+        def gather_scales(s):
             lo, n = SLICES[s]
-            scales_tag, codes_tag = GATHER_TAGS[s]
-            s_scales.append(keep.tile([128, n], U8, name=f"s_scales{lo}", tag=scales_tag, align_bytes=64))
-            s_codes.append(keep.tile([128, n], U32, name=f"s_codes{lo}", tag=codes_tag, align_bytes=64))
-            cols = offs_t[:, lo // 16 : (lo + n) // 16]
-            nc.vector.tensor_copy(s_scales[s][:], x_scales[:].indirect(cols))
-            nc.vector.tensor_copy(s_codes[s][:], x_codes[:].indirect(cols))
+            s_scales.append(keep.tile([128, n], U8, name=f"s_scales{lo}", tag=GATHER_TAGS[s][0], align_bytes=64))
+            nc.vector.tensor_copy(s_scales[s][:], x_scales[:].indirect(offs_t[:, lo // 16 : (lo + n) // 16]))
+
+        def gather_codes(s):
+            lo, n = SLICES[s]
+            s_codes.append(keep.tile([128, n], U32, name=f"s_codes{lo}", tag=GATHER_TAGS[s][1], align_bytes=64))
+            nc.vector.tensor_copy(s_codes[s][:], x_codes[:].indirect(offs_t[:, lo // 16 : (lo + n) // 16]))
 
         w_grouped = [keep.tile([128, 2, 1024], BF16, name=f"w_grouped{g}", tag=f"w_grouped{g}", align_bytes=64) for g in range(8)]
         w_codes = [keep.tile([128, 2, N], U32, name=f"w_codes{g}", align_bytes=64) for g in range(8)]
@@ -116,7 +120,8 @@ def tile_routed_moe_kernel(tc, xT, w, b, gate, offs, pos1, pos2, out):
         def interleave_w(e):
             g, j = divmod(e, 2)
             interleave(nc.vector.tensor_copy, w_grouped[g][:, j], w_raw[g][:, j], 0, VCOLS[e])
-            interleave(gpsimd_copy(nc), w_grouped[g][:, j], w_raw[g][:, j], VCOLS[e], VCOLS[e] + GCOLS[e])
+            for lo in range(0, GCOLS[e], 64):
+                interleave(gpsimd_copy(nc), w_grouped[g][:, j], w_raw[g][:, j], lo, lo + 64)
             interleave(nc.scalar.copy, w_grouped[g][:, j], w_raw[g][:, j], VCOLS[e] + GCOLS[e], N)
 
         def quantize_w(g):
@@ -169,13 +174,16 @@ def tile_routed_moe_kernel(tc, xT, w, b, gate, offs, pos1, pos2, out):
             quantize_x(i)
         for e in range(0, 8):
             interleave_w(e)
-        gather(0)
+        gather_scales(0)
+        gather_codes(0)
         quantize_w(0)
+        gather_scales(1)
         quantize_w(1)
-        gather(1)
+        gather_codes(1)
         quantize_w(2)
+        gather_scales(2)
         quantize_w(3)
-        gather(2)
+        gather_codes(2)
         for e in range(8, 16):
             interleave_w(e)
         for g in range(4, 8):

@@ -1,6 +1,13 @@
 import concourse.mybir as mybir
+from concourse.masks import make_identity
 
-FLOPS = 2 * 2048 * 512 * 256
+K, T, E, C, N = 512, 1024, 16, 128, 256
+SLOTS = E * C
+FLOPS = 2 * SLOTS * K * N
+
+P = 128
+PACK = 4
+PAIRS = E // 2
 
 F32 = mybir.dt.float32
 BF16 = mybir.dt.bfloat16
@@ -8,31 +15,29 @@ U32 = mybir.dt.uint32
 U16 = mybir.dt.uint16
 U8 = mybir.dt.uint8
 FP8X4 = mybir.dt.float8_e4m3fn_x4
-MULT = mybir.AluOpType.mult
 ADD = mybir.AluOpType.add
+MULT = mybir.AluOpType.mult
 IDENTITY = mybir.ActivationFunctionType.Identity
 
-K, T, E, C, N = 512, 1024, 16, 128, 256
-SLOTS = E * C
-VCOLS = [0,0,0,0,0,0,0,0,0,0,0,0,0,128,0,160]
-GCOLS = [0,0,256,0,0,0,256,0,0,0,256,0,0,0,0,0]
-X_PARTS = ((0, 512), (512, 512))
-XV = 320
-GATHER_TAGS = (("scales0", "codes0"), ("w_grouped0", "w_grouped1"), ("w_grouped2", "w_grouped3"))
-VECTOR_EMPTIES = ((7, 0),)
-SLICES = ((0, 768), (768, 768), (1536, 512))
+TOKEN_PARTS = ((0, 512, 320), (512, 256, 256), (768, 256, 256))
+
+VECTOR_COLUMNS = {11: 256, 12: 96, 13: 256, 15: 160}
+
+SLOT_PARTS = ((0, 768), (768, 768), (1536, 512))
+
+TENSOR_SUMS = ((0, 512), (512, 256))
+
+
+def members_of_pair(together):
+    return ((0, 2),) if together else ((0, 1), (1, 2))
 
 
 def interleave(copy, grouped, raw, lo, hi):
-    if hi > lo:
+    if lo < hi:
         copy(
-            grouped[:, 4 * lo : 4 * hi].rearrange("p (c i t) -> p c t i", i=4, t=4),
+            grouped[:, PACK * lo : PACK * hi].rearrange("p (c i t) -> p c t i", i=4, t=PACK),
             raw[:, :, lo:hi].rearrange("p t (c i) -> p c t i", i=4),
         )
-
-
-def gpsimd_copy(nc):
-    return lambda dst, src: nc.gpsimd.tensor_scalar(dst, src, 1.0, 0.0, MULT, ADD)
 
 
 def tile_routed_moe_kernel(tc, xT, w, b, gate, offs, pos1, pos2, out):
@@ -42,178 +47,165 @@ def tile_routed_moe_kernel(tc, xT, w, b, gate, offs, pos1, pos2, out):
         tc.tile_pool(name="keep", bufs=1) as keep,
         tc.psum_pool(name="psum", bufs=1) as psum,
     ):
-        offs_t = lists.tile([128, SLOTS // 16], U16, name="offs_t")
-        pos1_t = lists.tile([128, T // 16], U16, name="pos1_t")
-        pos2_t = lists.tile([128, T // 16], U16, name="pos2_t")
+        offs_list = lists.tile([P, SLOTS // 16], U16, name="offs_list")
+        pos1_list = lists.tile([P, T // 16], U16, name="pos1_list")
+        pos2_list = lists.tile([P, T // 16], U16, name="pos2_list")
 
-        x_codes = keep.tile([128, T], U32, name="x_codes", align_bytes=64)
-        x_scales = keep.tile([128, T], U8, name="x_scales", align_bytes=64)
+        x_codes = keep.tile([P, T], U32, name="x_codes", align_bytes=64)
+        x_scales = keep.tile([P, T], U8, name="x_scales", align_bytes=64)
         nc.gpsimd.memset(x_scales[:], 0)
+        identity = keep.tile([P, P], F32, name="identity")
+        make_identity(nc, identity[:])
 
-        w_raw = [keep.tile([128, 2, 4, N], F32, name=f"w_raw{g}") for g in range(8)]
+        x_raw = [keep.tile([P, PACK, n], F32, name=f"x_raw{lo}") for lo, n, on_vector in TOKEN_PARTS]
+        for raw, (lo, n, on_vector) in zip(x_raw, TOKEN_PARTS):
+            nc.sync.dma_start(out=raw[:], in_=xT.rearrange("(p t) n -> p t n", t=PACK)[:, :, lo : lo + n])
+        nc.sync.dma_start(offs_list[:], offs)
 
-        def load_w(g, lo, hi):
-            nc.sync.dma_start(
-                out=w_raw[g][:, lo:hi].rearrange("p e t n -> p e (t n)"),
-                in_=w[2 * g + lo : 2 * g + hi].rearrange("e (p t) n -> p e (t n)", t=4),
-            )
-
-        x_raw = [keep.tile([128, 4, n], F32, name=f"x_raw{lo}") for lo, n in X_PARTS]
-        for i, (lo, n) in enumerate(X_PARTS):
-            nc.sync.dma_start(out=x_raw[i][:], in_=xT.rearrange("(p t) n -> p t n", t=4)[:, :, lo : lo + n])
-        nc.sync.dma_start(offs_t[:], offs)
-        load_w(0, 0, 1)
-        load_w(0, 1, 2)
-        b_t = [keep.tile([128, 2, 8], F32, name=f"b_t{i}") for i in range(2)]
-        def load_bias(i):
-            nc.sync.dma_start(out=b_t[i][:], in_=b.rearrange("(h p) e -> p h e", h=2)[:, :, 8 * i : 8 * i + 8])
-
-        for g in range(1, 5):
-            load_w(g, 0, 2)
-        load_bias(0)
-        nc.sync.dma_start(pos1_t[:], pos1)
-        nc.sync.dma_start(pos2_t[:], pos2)
-        load_w(5, 0, 2)
-        load_w(6, 0, 1)
-        load_w(6, 1, 2)
-        load_w(7, 0, 1)
-        load_bias(1)
-        load_w(7, 1, 2)
-        gates = [[keep.tile([128, T], F32, name=f"gate{r}{h}") for r in range(2)] for h in range(2)]
+        w_raw = [keep.tile([P, 2, PACK, N], F32, name=f"w_raw{g}") for g in range(PAIRS)]
+        bias = keep.tile([P, 2, E], F32, name="bias")
+        for g in range(PAIRS):
+            for j0, j1 in members_of_pair(together=2 <= g < PAIRS - 2):
+                nc.sync.dma_start(
+                    out=w_raw[g][:, j0:j1].rearrange("p e t n -> p e (t n)"),
+                    in_=w[2 * g + j0 : 2 * g + j1].rearrange("e (p t) n -> p e (t n)", t=PACK),
+                )
+            if g == PAIRS - 2:
+                nc.sync.dma_start(out=bias[:], in_=b.rearrange("(h p) e -> p h e", h=2))
+        nc.sync.dma_start(pos1_list[:], pos1)
+        nc.sync.dma_start(pos2_list[:], pos2)
+        gates = [[keep.tile([P, T], F32, name=f"gate{h}{r}") for r in range(2)] for h in range(2)]
         for h in range(2):
             for r in range(2):
-                nc.sync.dma_start(out=gates[h][r][:], in_=gate[r, 128 * h : 128 * (h + 1), :])
+                nc.sync.dma_start(out=gates[h][r][:], in_=gate[r, P * h : P * (h + 1), :])
 
-        x_grouped = [keep.tile([128, 4 * n], BF16, name=f"x_grouped{lo}", align_bytes=64) for lo, n in X_PARTS]
-
-        def interleave_x(i):
-            lo, n = X_PARTS[i]
-            part = x_raw[i]
-            interleave(nc.vector.tensor_copy, x_grouped[i], part, 0, XV * n // 512)
-            interleave(nc.scalar.copy, x_grouped[i], part, XV * n // 512, n)
-
-        def quantize_x(i):
-            lo, n = X_PARTS[i]
+        x_grouped = [
+            keep.tile([P, PACK * n], BF16, name=f"x_grouped{lo}", align_bytes=64) for lo, n, on_vector in TOKEN_PARTS
+        ]
+        for grouped, raw, (lo, n, on_vector) in zip(x_grouped, x_raw, TOKEN_PARTS):
+            interleave(nc.vector.tensor_copy, grouped, raw, 0, on_vector)
+            interleave(nc.scalar.copy, grouped, raw, on_vector, n)
+        for grouped, (lo, n, on_vector) in zip(x_grouped, TOKEN_PARTS):
             nc.vector.quantize_mx(
-                out=x_codes[:, lo : lo + n].bitcast(FP8X4), scales=x_scales[:, lo : lo + n], in_=x_grouped[i][:]
+                out=x_codes[:, lo : lo + n].bitcast(FP8X4), scales=x_scales[:, lo : lo + n], in_=grouped[:]
             )
 
-        y = [keep.tile([128, SLOTS], F32, name=f"y{h}") for h in range(2)]
-        s_codes = []
-        s_scales = []
+        w_grouped = [keep.tile([P, 2, PACK * N], BF16, name=f"w_grouped{g}", align_bytes=64) for g in range(PAIRS)]
+        w_codes = [keep.tile([P, 2, N], U32, name=f"w_codes{g}", align_bytes=64) for g in range(PAIRS)]
+        w_scales = [keep.tile([P, 2, N], U8, name=f"w_scales{g}", align_bytes=64) for g in range(PAIRS)]
 
-        def gather_scales(s):
-            lo, n = SLICES[s]
-            s_scales.append(keep.tile([128, n], U8, name=f"s_scales{lo}", tag=GATHER_TAGS[s][0], align_bytes=64))
-            nc.vector.tensor_copy(s_scales[s][:], x_scales[:].indirect(offs_t[:, lo // 16 : (lo + n) // 16]))
-
-        def gather_codes(s):
-            lo, n = SLICES[s]
-            s_codes.append(keep.tile([128, n], U32, name=f"s_codes{lo}", tag=GATHER_TAGS[s][1], align_bytes=64))
-            nc.vector.tensor_copy(s_codes[s][:], x_codes[:].indirect(offs_t[:, lo // 16 : (lo + n) // 16]))
-
-        w_grouped = [keep.tile([128, 2, 1024], BF16, name=f"w_grouped{g}", tag=f"w_grouped{g}", align_bytes=64) for g in range(8)]
-        w_codes = [keep.tile([128, 2, N], U32, name=f"w_codes{g}", align_bytes=64) for g in range(8)]
-        w_scales = [keep.tile([128, 2, N], U8, name=f"w_scales{g}", align_bytes=64) for g in range(8)]
-        sums = [psum.tile([128, 2, 2, C], F32, name=f"sums{g}") for g in range(8)]
-
-        def interleave_w(e):
+        def interleave_weights(e):
             g, j = divmod(e, 2)
-            interleave(nc.vector.tensor_copy, w_grouped[g][:, j], w_raw[g][:, j], 0, VCOLS[e])
-            for lo in range(0, GCOLS[e], 64):
-                interleave(gpsimd_copy(nc), w_grouped[g][:, j], w_raw[g][:, j], lo, lo + 64)
-            interleave(nc.scalar.copy, w_grouped[g][:, j], w_raw[g][:, j], VCOLS[e] + GCOLS[e], N)
+            on_vector = VECTOR_COLUMNS.get(e, 0)
+            interleave(nc.vector.tensor_copy, w_grouped[g][:, j], w_raw[g][:, j], 0, on_vector)
+            interleave(nc.scalar.copy, w_grouped[g][:, j], w_raw[g][:, j], on_vector, N)
 
-        def quantize_w(g):
-            if g < 7:
+        def quantize_weights(g):
+            for j0, j1 in members_of_pair(together=g < PAIRS - 1):
                 nc.vector.quantize_mx(
-                    out=w_codes[g][:].rearrange("p e n -> p (e n)").bitcast(FP8X4),
-                    scales=w_scales[g][:].rearrange("p e n -> p (e n)"),
-                    in_=w_grouped[g][:].rearrange("p e k -> p (e k)"),
+                    out=w_codes[g][:, j0:j1].rearrange("p e n -> p (e n)").bitcast(FP8X4),
+                    scales=w_scales[g][:, j0:j1].rearrange("p e n -> p (e n)"),
+                    in_=w_grouped[g][:, j0:j1].rearrange("p e k -> p (e k)"),
                 )
-            else:
-                for j in range(2):
-                    nc.vector.quantize_mx(
-                        out=w_codes[g][:, j].bitcast(FP8X4), scales=w_scales[g][:, j], in_=w_grouped[g][:, j]
-                    )
+
+        s_codes = [keep.tile([P, n], U32, name=f"s_codes{lo}", align_bytes=64) for lo, n in SLOT_PARTS]
+        s_scales = [keep.tile([P, n], U8, name=f"s_scales{lo}", align_bytes=64) for lo, n in SLOT_PARTS]
+
+        def gather_slots(s):
+            lo, n = SLOT_PARTS[s]
+            idx = offs_list[:, lo // 16 : (lo + n) // 16]
+            nc.vector.tensor_copy(s_scales[s][:], x_scales[:].indirect(idx))
+            nc.vector.tensor_copy(s_codes[s][:], x_codes[:].indirect(idx))
+
+        sums = [psum.tile([P, 2, 2, C], F32, name=f"sums{g}", tag=f"bank{g}") for g in range(PAIRS)]
 
         def multiply(g):
             for j in range(2):
-                e = 2 * g + j
-                s = [lo <= e * C < lo + n for lo, n in SLICES].index(True)
-                c0 = e * C - SLICES[s][0]
+                first_slot = (2 * g + j) * C
+                s = [lo <= first_slot < lo + n for lo, n in SLOT_PARTS].index(True)
+                slots = slice(first_slot - SLOT_PARTS[s][0], first_slot - SLOT_PARTS[s][0] + C)
                 for h in range(2):
+                    features = slice(P * h, P * (h + 1))
                     nc.tensor.matmul_mx(
                         out=sums[g][:, j, h, :],
-                        lhsT=w_codes[g][:, j, 128 * h : 128 * (h + 1)].bitcast(FP8X4),
-                        lhsT_scale=w_scales[g][:, j, 128 * h : 128 * (h + 1)],
-                        rhs=s_codes[s][:, c0 : c0 + C].bitcast(FP8X4),
-                        rhs_scale=s_scales[s][:, c0 : c0 + C],
+                        lhsT=w_codes[g][:, j, features].bitcast(FP8X4),
+                        lhsT_scale=w_scales[g][:, j, features],
+                        rhs=s_codes[s][:, slots].bitcast(FP8X4),
+                        rhs_scale=s_scales[s][:, slots],
                         start=True,
                         stop=True,
                     )
 
-        def empty(g, h):
-            y_pair = y[h][:, 2 * g * C : 2 * (g + 1) * C]
-            if (g, h) in VECTOR_EMPTIES:
+        y = [keep.tile([P, SLOTS], F32, name=f"y{h}") for h in range(2)]
+
+        def add_bias(g, h):
+            if (g, h) == (PAIRS - 1, 0):
                 nc.vector.tensor_tensor(
-                    y_pair.rearrange("p (e c) -> p e c", c=C),
+                    y[h][:, 2 * g * C : 2 * (g + 1) * C].rearrange("p (e c) -> p e c", c=C),
                     sums[g][:, :, h, :],
-                    b_t[g // 4][:, h, 2 * g % 8 : 2 * g % 8 + 2].unsqueeze(2).to_broadcast([128, 2, C]),
+                    bias[:, h, 2 * g : 2 * g + 2].unsqueeze(2).to_broadcast([P, 2, C]),
                     ADD,
                 )
                 return
             for j in range(2):
                 e = 2 * g + j
                 nc.scalar.activation(
-                    y[h][:, e * C : (e + 1) * C], sums[g][:, j, h, :], IDENTITY, bias=b_t[g // 4][:, h, e % 8 : e % 8 + 1]
+                    y[h][:, e * C : (e + 1) * C], sums[g][:, j, h, :], IDENTITY, bias=bias[:, h, e : e + 1]
                 )
 
-        for i in range(len(X_PARTS)):
-            interleave_x(i)
-            quantize_x(i)
-        for e in range(0, 8):
-            interleave_w(e)
-        gather_scales(0)
-        gather_codes(0)
-        quantize_w(0)
-        gather_scales(1)
-        quantize_w(1)
-        gather_codes(1)
-        quantize_w(2)
-        gather_scales(2)
-        quantize_w(3)
-        gather_codes(2)
-        for e in range(8, 16):
-            interleave_w(e)
-        for g in range(4, 8):
-            quantize_w(g)
-        for g in range(0, 8):
+        for e in range(E // 2):
+            interleave_weights(e)
+        gather_slots(0)
+        quantize_weights(0)
+        quantize_weights(1)
+        gather_slots(1)
+        quantize_weights(2)
+        quantize_weights(3)
+        gather_slots(2)
+        for e in range(E // 2, E):
+            interleave_weights(e)
+        for g in range(4, PAIRS):
+            quantize_weights(g)
+        for g in range(PAIRS):
             multiply(g)
         for h in range(2):
-            for g in range(0, 8):
-                empty(g, h)
+            for g in range(PAIRS):
+                add_bias(g, h)
 
-        parts = [[keep.tile([128, T], F32, name=f"part{h}{r}") for r in range(2)] for h in range(2)]
-        result = [keep.tile([128, T], F32, name=f"result{h}") for h in range(2)]
+        products = [[keep.tile([P, T], F32, name=f"product{h}{r}") for r in range(2)] for h in range(2)]
+        result = [keep.tile([P, T], F32, name=f"result{h}") for h in range(2)]
 
-        def combine(h, lo, n):
-            for r, pos_t in enumerate((pos1_t, pos2_t)):
+        def multiply_by_gate(h, lo, n):
+            tokens = slice(lo, lo + n)
+            for r, pos in enumerate((pos1_list, pos2_list)):
                 nc.vector.tensor_tensor(
-                    parts[h][r][:, lo : lo + n],
-                    y[h][:].indirect(pos_t[:, lo // 16 : (lo + n) // 16]),
-                    gates[h][r][:, lo : lo + n],
+                    products[h][r][:, tokens],
+                    y[h][:].indirect(pos[:, lo // 16 : (lo + n) // 16]),
+                    gates[h][r][:, tokens],
                     MULT,
                 )
 
-        def finish(h, lo, n):
-            cols = slice(lo, lo + n)
-            nc.vector.tensor_tensor(result[h][:, cols], parts[h][0][:, cols], parts[h][1][:, cols], ADD)
-            nc.sync.dma_start(out=out[128 * h : 128 * (h + 1), cols], in_=result[h][:, cols])
+        def store(h, tokens):
+            nc.sync.dma_start(out=out[P * h : P * (h + 1), tokens], in_=result[h][:, tokens])
 
-        combine(0, 0, 1024)
-        combine(1, 0, 512)
-        finish(0, 0, 1024)
-        combine(1, 512, 512)
-        finish(1, 0, 512)
-        finish(1, 512, 512)
+        def sum_on_tensor(bank, h, lo, n):
+            tokens = slice(lo, lo + n)
+            total = psum.tile([P, n], F32, name=f"total{lo}", tag=f"bank{bank}")
+            for r in range(2):
+                nc.tensor.matmul(total[:], identity[:], products[h][r][:, tokens], start=r == 0, stop=r == 1)
+            nc.scalar.copy(result[h][:, tokens], total[:])
+            store(h, tokens)
+
+        def sum_on_vector(h, lo, n):
+            tokens = slice(lo, lo + n)
+            nc.vector.tensor_tensor(result[h][:, tokens], products[h][0][:, tokens], products[h][1][:, tokens], ADD)
+            store(h, tokens)
+
+        multiply_by_gate(0, 0, T)
+        multiply_by_gate(1, 0, T // 2)
+        for bank, (lo, n) in enumerate(TENSOR_SUMS):
+            sum_on_tensor(bank, 0, lo, n)
+        sum_on_vector(0, 768, 256)
+        multiply_by_gate(1, T // 2, T // 2)
+        sum_on_vector(1, 0, T // 2)
+        sum_on_vector(1, T // 2, T // 2)

import concourse.mybir as mybir
from concourse.masks import make_identity

K, T, E, C, N = 512, 1024, 16, 128, 256
SLOTS = E * C
FLOPS = 2 * SLOTS * K * N

P = 128
PACK = 4
PAIRS = E // 2

F32 = mybir.dt.float32
BF16 = mybir.dt.bfloat16
U32 = mybir.dt.uint32
U16 = mybir.dt.uint16
U8 = mybir.dt.uint8
FP8X4 = mybir.dt.float8_e4m3fn_x4
ADD = mybir.AluOpType.add
MULT = mybir.AluOpType.mult
IDENTITY = mybir.ActivationFunctionType.Identity

TOKEN_PARTS = ((0, 512, 320), (512, 256, 256), (768, 256, 256))

VECTOR_COLUMNS = {11: 256, 12: 96, 13: 256, 15: 160}

SLOT_PARTS = ((0, 768), (768, 768), (1536, 512))

TENSOR_SUMS = ((0, 512), (512, 256))


def members_of_pair(together):
    return ((0, 2),) if together else ((0, 1), (1, 2))


def interleave(copy, grouped, raw, lo, hi):
    if lo < hi:
        copy(
            grouped[:, PACK * lo : PACK * hi].rearrange("p (c i t) -> p c t i", i=4, t=PACK),
            raw[:, :, lo:hi].rearrange("p t (c i) -> p c t i", i=4),
        )


def tile_routed_moe_kernel(tc, xT, w, b, gate, offs, pos1, pos2, out):
    nc = tc.nc
    with (
        tc.tile_pool(name="lists", bufs=1) as lists,
        tc.tile_pool(name="keep", bufs=1) as keep,
        tc.psum_pool(name="psum", bufs=1) as psum,
    ):
        offs_list = lists.tile([P, SLOTS // 16], U16, name="offs_list")
        pos1_list = lists.tile([P, T // 16], U16, name="pos1_list")
        pos2_list = lists.tile([P, T // 16], U16, name="pos2_list")

        x_codes = keep.tile([P, T], U32, name="x_codes", align_bytes=64)
        x_scales = keep.tile([P, T], U8, name="x_scales", align_bytes=64)
        nc.gpsimd.memset(x_scales[:], 0)
        identity = keep.tile([P, P], F32, name="identity")
        make_identity(nc, identity[:])

        x_raw = [keep.tile([P, PACK, n], F32, name=f"x_raw{lo}") for lo, n, on_vector in TOKEN_PARTS]
        for raw, (lo, n, on_vector) in zip(x_raw, TOKEN_PARTS):
            nc.sync.dma_start(out=raw[:], in_=xT.rearrange("(p t) n -> p t n", t=PACK)[:, :, lo : lo + n])
        nc.sync.dma_start(offs_list[:], offs)

        w_raw = [keep.tile([P, 2, PACK, N], F32, name=f"w_raw{g}") for g in range(PAIRS)]
        bias = keep.tile([P, 2, E], F32, name="bias")
        for g in range(PAIRS):
            for j0, j1 in members_of_pair(together=2 <= g < PAIRS - 2):
                nc.sync.dma_start(
                    out=w_raw[g][:, j0:j1].rearrange("p e t n -> p e (t n)"),
                    in_=w[2 * g + j0 : 2 * g + j1].rearrange("e (p t) n -> p e (t n)", t=PACK),
                )
            if g == PAIRS - 2:
                nc.sync.dma_start(out=bias[:], in_=b.rearrange("(h p) e -> p h e", h=2))
        nc.sync.dma_start(pos1_list[:], pos1)
        nc.sync.dma_start(pos2_list[:], pos2)
        gates = [[keep.tile([P, T], F32, name=f"gate{h}{r}") for r in range(2)] for h in range(2)]
        for h in range(2):
            for r in range(2):
                nc.sync.dma_start(out=gates[h][r][:], in_=gate[r, P * h : P * (h + 1), :])

        x_grouped = [
            keep.tile([P, PACK * n], BF16, name=f"x_grouped{lo}", align_bytes=64) for lo, n, on_vector in TOKEN_PARTS
        ]
        for grouped, raw, (lo, n, on_vector) in zip(x_grouped, x_raw, TOKEN_PARTS):
            interleave(nc.vector.tensor_copy, grouped, raw, 0, on_vector)
            interleave(nc.scalar.copy, grouped, raw, on_vector, n)
        for grouped, (lo, n, on_vector) in zip(x_grouped, TOKEN_PARTS):
            nc.vector.quantize_mx(
                out=x_codes[:, lo : lo + n].bitcast(FP8X4), scales=x_scales[:, lo : lo + n], in_=grouped[:]
            )

        w_grouped = [keep.tile([P, 2, PACK * N], BF16, name=f"w_grouped{g}", align_bytes=64) for g in range(PAIRS)]
        w_codes = [keep.tile([P, 2, N], U32, name=f"w_codes{g}", align_bytes=64) for g in range(PAIRS)]
        w_scales = [keep.tile([P, 2, N], U8, name=f"w_scales{g}", align_bytes=64) for g in range(PAIRS)]

        def interleave_weights(e):
            g, j = divmod(e, 2)
            on_vector = VECTOR_COLUMNS.get(e, 0)
            interleave(nc.vector.tensor_copy, w_grouped[g][:, j], w_raw[g][:, j], 0, on_vector)
            interleave(nc.scalar.copy, w_grouped[g][:, j], w_raw[g][:, j], on_vector, N)

        def quantize_weights(g):
            for j0, j1 in members_of_pair(together=g < PAIRS - 1):
                nc.vector.quantize_mx(
                    out=w_codes[g][:, j0:j1].rearrange("p e n -> p (e n)").bitcast(FP8X4),
                    scales=w_scales[g][:, j0:j1].rearrange("p e n -> p (e n)"),
                    in_=w_grouped[g][:, j0:j1].rearrange("p e k -> p (e k)"),
                )

        s_codes = [keep.tile([P, n], U32, name=f"s_codes{lo}", align_bytes=64) for lo, n in SLOT_PARTS]
        s_scales = [keep.tile([P, n], U8, name=f"s_scales{lo}", align_bytes=64) for lo, n in SLOT_PARTS]

        def gather_slots(s):
            lo, n = SLOT_PARTS[s]
            idx = offs_list[:, lo // 16 : (lo + n) // 16]
            nc.vector.tensor_copy(s_scales[s][:], x_scales[:].indirect(idx))
            nc.vector.tensor_copy(s_codes[s][:], x_codes[:].indirect(idx))

        sums = [psum.tile([P, 2, 2, C], F32, name=f"sums{g}", tag=f"bank{g}") for g in range(PAIRS)]

        def multiply(g):
            for j in range(2):
                first_slot = (2 * g + j) * C
                s = [lo <= first_slot < lo + n for lo, n in SLOT_PARTS].index(True)
                slots = slice(first_slot - SLOT_PARTS[s][0], first_slot - SLOT_PARTS[s][0] + C)
                for h in range(2):
                    features = slice(P * h, P * (h + 1))
                    nc.tensor.matmul_mx(
                        out=sums[g][:, j, h, :],
                        lhsT=w_codes[g][:, j, features].bitcast(FP8X4),
                        lhsT_scale=w_scales[g][:, j, features],
                        rhs=s_codes[s][:, slots].bitcast(FP8X4),
                        rhs_scale=s_scales[s][:, slots],
                        start=True,
                        stop=True,
                    )

        y = [keep.tile([P, SLOTS], F32, name=f"y{h}") for h in range(2)]

        def add_bias(g, h):
            if (g, h) == (PAIRS - 1, 0):
                nc.vector.tensor_tensor(
                    y[h][:, 2 * g * C : 2 * (g + 1) * C].rearrange("p (e c) -> p e c", c=C),
                    sums[g][:, :, h, :],
                    bias[:, h, 2 * g : 2 * g + 2].unsqueeze(2).to_broadcast([P, 2, C]),
                    ADD,
                )
                return
            for j in range(2):
                e = 2 * g + j
                nc.scalar.activation(
                    y[h][:, e * C : (e + 1) * C], sums[g][:, j, h, :], IDENTITY, bias=bias[:, h, e : e + 1]
                )

        for e in range(E // 2):
            interleave_weights(e)
        gather_slots(0)
        quantize_weights(0)
        quantize_weights(1)
        gather_slots(1)
        quantize_weights(2)
        quantize_weights(3)
        gather_slots(2)
        for e in range(E // 2, E):
            interleave_weights(e)
        for g in range(4, PAIRS):
            quantize_weights(g)
        for g in range(PAIRS):
            multiply(g)
        for h in range(2):
            for g in range(PAIRS):
                add_bias(g, h)

        products = [[keep.tile([P, T], F32, name=f"product{h}{r}") for r in range(2)] for h in range(2)]
        result = [keep.tile([P, T], F32, name=f"result{h}") for h in range(2)]

        def multiply_by_gate(h, lo, n):
            tokens = slice(lo, lo + n)
            for r, pos in enumerate((pos1_list, pos2_list)):
                nc.vector.tensor_tensor(
                    products[h][r][:, tokens],
                    y[h][:].indirect(pos[:, lo // 16 : (lo + n) // 16]),
                    gates[h][r][:, tokens],
                    MULT,
                )

        def store(h, tokens):
            nc.sync.dma_start(out=out[P * h : P * (h + 1), tokens], in_=result[h][:, tokens])

        def sum_on_tensor(bank, h, lo, n):
            tokens = slice(lo, lo + n)
            total = psum.tile([P, n], F32, name=f"total{lo}", tag=f"bank{bank}")
            for r in range(2):
                nc.tensor.matmul(total[:], identity[:], products[h][r][:, tokens], start=r == 0, stop=r == 1)
            nc.scalar.copy(result[h][:, tokens], total[:])
            store(h, tokens)

        def sum_on_vector(h, lo, n):
            tokens = slice(lo, lo + n)
            nc.vector.tensor_tensor(result[h][:, tokens], products[h][0][:, tokens], products[h][1][:, tokens], ADD)
            store(h, tokens)

        multiply_by_gate(0, 0, T)
        multiply_by_gate(1, 0, T // 2)
        for bank, (lo, n) in enumerate(TENSOR_SUMS):
            sum_on_tensor(bank, 0, lo, n)
        sum_on_vector(0, 768, 256)
        multiply_by_gate(1, T // 2, T // 2)
        sum_on_vector(1, 0, T // 2)
        sum_on_vector(1, T // 2, T // 2)
